import numpy as np
import ml_dtypes


def mxq(x, axis, fmt="e4m3"):
    dtype, down = {"e4m3": (ml_dtypes.float8_e4m3fn, 7), "e5m2": (ml_dtypes.float8_e5m2, 14)}[fmt]
    v = np.moveaxis(np.asarray(x, np.float32).astype(ml_dtypes.bfloat16).astype(np.float64), axis, -1)
    blocks = v.reshape(v.shape[:-1] + (-1, 32))
    amax = np.abs(blocks).max(-1, keepdims=True)
    byte = np.maximum(np.where(amax > 0, np.frexp(amax)[1] - 1 + 127, 0) - down, 1)
    scale = np.exp2(byte - 127.0)
    codes = (blocks / scale).astype(np.float32).astype(dtype).astype(np.float64)
    return np.moveaxis((codes * scale).reshape(v.shape), -1, axis)


WIDE = False


def mx_kscale(k):
    if not WIDE:
        return np.ones(k)
    levels = np.array([10, -10, 5, -5, 0])
    if k % 512:
        return np.exp2(np.random.permutation(np.resize(levels, k // 32))).repeat(32)
    a = np.empty((k // 512, 16))
    for p in range(k // 512):
        a[p, :8] = np.random.permutation(np.resize(levels, 8))
        for g in range(8):
            far = levels[np.abs(levels - a[p, g]) >= 10]
            a[p, g + 8] = far[np.random.randint(len(far))]
    return np.exp2(a.ravel()).repeat(32)


def f64(x):
    return np.asarray(x).astype(np.float64)


def striped(idx):
    return np.tile(idx.reshape(-1, 16).T, (8, 1)).astype(np.uint16)


def unstriped(offs):
    return offs[:16].T.reshape(-1).astype(np.int64)


def pack_weight(w):
    k, n = w.shape
    w = f64(np.asarray(w, np.float32).astype(ml_dtypes.bfloat16)).reshape(k // 32, 32, n)
    amax = np.abs(w).max(1)
    byte = np.clip(np.where(amax > 0, np.frexp(amax)[1] - 1 + 127 - 7, 1), 1, 254)
    scaled = (w * np.exp2(127.0 - byte)[:, None, :]).reshape(k, n).astype(np.float32)
    words = np.ascontiguousarray(scaled.reshape(k // 512, 128, 4, n).transpose(0, 1, 3, 2)).astype(ml_dtypes.float8_e4m3fn).view(np.uint8)
    return words, np.ascontiguousarray(byte.astype(np.uint8).reshape(k // 512, 16, n))


def unpack_weight(words, scales):
    g, p, n, _ = words.shape
    vals = np.ascontiguousarray(words).view(ml_dtypes.float8_e4m3fn).astype(np.float64) * np.repeat(np.exp2(scales.astype(np.float64) - 127.0), 8, axis=1)[..., None]
    return vals.transpose(0, 1, 3, 2).reshape(g * 512, n)


def sigmoid(v):
    return 1.0 / (1.0 + np.exp(-np.maximum(v, -700.0)))


K, T, S, H, G, V = 512, 2048, 512, 512, 1024, 512
P = 2 ** 7


def setup_inputs():
    n = np.random.standard_normal
    s = mx_kscale(K)[:, None]
    u = mx_kscale(H)
    packed_xT = pack_weight(n((K, T)) * s)
    packed_vT = pack_weight(n((H, G)) / np.sqrt(H) / u[:, None])
    packed_gT = pack_weight(n((H, G)) / np.sqrt(H) / u[:, None])
    return {
        "x_words": packed_xT[0],
        "x_scales": packed_xT[1],
        "w1": (n((K, H)) / np.sqrt(K) / s).astype(np.float32),
        "wpos": (np.random.uniform(0.5, 1.5, (H, 1)) * u[:, None]).astype(np.float32),
        "wneg": (np.random.uniform(0.5, 1.5, (H, 1)) * u[:, None]).astype(np.float32),
        "v_words": packed_vT[0],
        "v_scales": packed_vT[1],
        "g_words": packed_gT[0],
        "g_scales": packed_gT[1],
        "prior": (np.tile(0.3 * n(G), (P, 1))).astype(np.float32),
        "offs": striped(np.random.permutation(T)[:S]),
        "cand": striped(np.random.permutation(G)[:V]),
    }


def reference(x_words, x_scales, w1, wpos, wneg, v_words, v_scales, g_words, g_scales, prior, offs, cand):
    xq = unpack_weight(x_words, x_scales)[:, unstriped(offs)]
    p = sigmoid(mxq(f64(w1), 0, "e4m3").T @ xq)
    lp = f64(wpos) * np.log(p + 0.02)
    v_cand = unpack_weight(v_words, v_scales)[:, unstriped(cand)]
    ln = f64(wneg) * np.log(-1.0 * p + 1.02)
    g_cand = unpack_weight(g_words, g_scales)[:, unstriped(cand)]
    y = (mxq(lp, 0, "e4m3").T @ v_cand + mxq(ln, 0, "e4m3").T @ g_cand) + f64(prior)[:1][:, unstriped(cand)]
    ex = np.exp(y - y.max(axis=1, keepdims=True))
    return ex / ex.sum(axis=1, keepdims=True)

@@ -1,0 +1,192 @@
+from contextlib import ExitStack
+
+import concourse.mybir as mybir
+
+F32 = mybir.dt.float32
+BF16 = mybir.dt.bfloat16
+I32 = mybir.dt.int32
+U32 = mybir.dt.uint32
+U16 = mybir.dt.uint16
+U8 = mybir.dt.uint8
+FP8X4 = mybir.dt.float8_e4m3fn_x4
+ACT = mybir.ActivationFunctionType
+ALU = mybir.AluOpType
+AXIS = mybir.AxisListType
+
+P = 128
+PACK = 4
+K, T, S, H, G, V = 512, 2048, 512, 512, 1024, 512
+ROWS = S // P
+HALF = S // 2
+
+FLOPS = 2 * K * H * S + 2 * 2 * H * S * V
+BYTES = 4 * (K * H + 2 * H + G + S * V) + (K + K // 32) * S + 2 * (H + H // 32) * V + 2 * (S + V)
+
+
+def tile_picked_ymolrank_post_p_kernel(
+    tc, x_words, x_scales, w1, wpos, wneg, v_words, v_scales, g_words, g_scales, prior, offs, cand, out
+):
+    nc = tc.nc
+    with ExitStack() as ctx:
+        keep = ctx.enter_context(tc.tile_pool(name="keep", bufs=1))
+        psum = ctx.enter_context(tc.psum_pool(name="psum", bufs=1))
+
+        def tile(shape, dtype, name, tag=None):
+            return keep.tile(shape, dtype, name=name, tag=tag or name, align_bytes=64)
+
+        offs_sb = tile([P, S // 16], U16, "offs_sb")
+        cand_sb = tile([P, V // 16], U16, "cand_sb")
+
+        def words_view(words):
+            return words[0].rearrange("p n t -> p (n t)").bitcast(I32)
+
+        def load_scale_rows(queues, table, scales):
+            for quad, queue in enumerate(queues):
+                queue.dma_start(
+                    out=table[32 * quad : 32 * quad + 4, :].bitcast(I32),
+                    in_=scales[0, 4 * quad : 4 * quad + 4, :].bitcast(I32),
+                )
+
+        def gather(name, table, offsets, count, dtype):
+            picked = tile([P, count], dtype, name)
+            nc.vector.tensor_copy(out=picked[:], in_=table[:].indirect(offsets))
+            return picked
+
+        xs_table = tile([P, T], U8, "xs_table", "scale_rows")
+        vs_table = tile([P, G], U8, "vs_table")
+        nc.gpsimd.memset(xs_table[:].bitcast(I32), 0)
+        nc.gpsimd.memset(vs_table[:].bitcast(I32), 0)
+
+        nc.sync.dma_start(out=offs_sb[:], in_=offs)
+        nc.sync.dma_start(out=cand_sb[:], in_=cand)
+        w1_rows = w1.rearrange("(p j) c -> p j c", j=PACK)
+        w_raw = [tile([P, PACK, H // 2], F32, f"w_raw{h}", f"stage{h}") for h in range(2)]
+        for h in range(2):
+            nc.scalar.dma_start(out=w_raw[h][:], in_=w1_rows[:, :, h * (H // 2) : (h + 1) * (H // 2)])
+        xw_table = tile([P, T], U32, "xw_table", "wide")
+        nc.scalar.dma_start(out=xw_table[:].bitcast(I32), in_=words_view(x_words))
+        load_scale_rows([nc.sync] * 4, xs_table, x_scales)
+        load_scale_rows([nc.gpsimd, nc.gpsimd, nc.sync, nc.sync], vs_table, v_scales)
+        wpos_sb = tile([P, PACK], F32, "wpos_sb")
+        wneg_sb = tile([P, PACK], F32, "wneg_sb")
+        nc.gpsimd.dma_start(out=wpos_sb[:], in_=wpos.rearrange("(p j) o -> p (j o)", j=PACK))
+        nc.gpsimd.dma_start(out=wneg_sb[:], in_=wneg.rearrange("(p j) o -> p (j o)", j=PACK))
+
+        warm = tile([P, 1], F32, "warm")
+        nc.vector.memset(warm[:], 0.0)
+        nc.scalar.activation(out=warm[:], in_=warm[:], func=ACT.Tanh)
+
+        xs = gather("xs", xs_table, offs_sb[:], S, U8)
+        vs = gather("vs", vs_table, cand_sb[:], V, U8)
+
+        w_grouped = tile([P, PACK, P, PACK], BF16, "w_grouped")
+        for h in range(2):
+            nc.scalar.copy(
+                out=w_grouped[:, :, h * (P // 2) : (h + 1) * (P // 2), :].rearrange("p t m j -> p m t j"),
+                in_=w_raw[h][:].rearrange("p j (m t) -> p m t j", t=PACK),
+            )
+        vw_table = tile([P, G], U32, "vw_table", "stage0")
+        nc.sync.dma_start(out=vw_table[:].bitcast(I32), in_=words_view(v_words))
+        gs_table = tile([P, G], U8, "gs_table", "scale_rows")
+        nc.gpsimd.memset(gs_table[:].bitcast(I32), 0)
+        load_scale_rows([nc.sync] * 4, gs_table, g_scales)
+        gw_table = tile([P, G], U32, "gw_table", "stage1")
+        nc.sync.dma_start(out=gw_table[:].bitcast(I32), in_=words_view(g_words))
+
+        w_codes = tile([P, H], U32, "w_codes")
+        w_scales = tile([P, H], U8, "w_scales")
+        nc.vector.quantize_mx(
+            out=w_codes[:].bitcast(FP8X4),
+            scales=w_scales[:],
+            in_=w_grouped[:].rearrange("p t m j -> p (t m j)"),
+        )
+
+        xw = [
+            gather(f"xw{h}", xw_table, offs_sb[:, h * (HALF // 16) : (h + 1) * (HALF // 16)], HALF, U32)
+            for h in range(2)
+        ]
+
+        prior_table = tile([P, G], F32, "prior_table", "wide")
+        nc.sync.dma_start(out=prior_table[:], in_=prior)
+
+        half_tanh = []
+        for r in range(ROWS):
+            z = psum.tile([P, PACK, P], F32, name=f"z{r}")
+            h, lo = divmod(r * P, HALF)
+            for t in range(PACK):
+                nc.tensor.matmul_mx(
+                    out=z[:, t, :],
+                    lhsT=w_codes[:, t * P : (t + 1) * P].bitcast(FP8X4),
+                    lhsT_scale=w_scales[:, t * P : (t + 1) * P],
+                    rhs=xw[h][:, lo : lo + P].bitcast(FP8X4),
+                    rhs_scale=xs[:, r * P : (r + 1) * P],
+                    start=True,
+                    stop=True,
+                )
+            th = tile([P, P, PACK], F32, f"th{r}")
+            nc.scalar.activation(out=th[:], in_=z[:].rearrange("p t n -> p n t"), func=ACT.Tanh, scale=0.5)
+            half_tanh.append(th)
+
+        gs = gather("gs", gs_table, cand_sb[:], V, U8)
+        vw = gather("vw", vw_table, cand_sb[:], V, U32)
+        gw = gather("gw", gw_table, cand_sb[:], V, U32)
+        prior_sb = gather("prior_sb", prior_table, cand_sb[:], V, F32)
+
+        sides = ((0.5, wpos_sb, vw, vs), (-0.5, wneg_sb, gw, gs))
+
+        def logs(r):
+            y = psum.tile([P, V], F32, name=f"y{r}")
+            rounded = []
+            for s, (slope, weight, words, scales) in enumerate(sides):
+                lg = tile([P, P, PACK], F32, f"log{r}_{s}")
+                nc.scalar.activation(out=lg[:], in_=half_tanh[r][:], func=ACT.Ln, scale=slope, bias=0.52)
+                lb = tile([P, P, PACK], BF16, f"lb{r}_{s}")
+                nc.vector.tensor_tensor(
+                    out=lb[:], in0=lg[:], in1=weight[:].unsqueeze(1).to_broadcast([P, P, PACK]), op=ALU.mult
+                )
+                rounded.append(lb)
+            for s, (slope, weight, words, scales) in enumerate(sides):
+                codes = tile([P, P], U32, f"lc{r}_{s}")
+                plane = tile([P, P], U8, f"ls{r}_{s}")
+                nc.vector.quantize_mx(
+                    out=codes[:].bitcast(FP8X4), scales=plane[:], in_=rounded[s][:].rearrange("p n t -> p (n t)")
+                )
+                nc.tensor.matmul_mx(
+                    out=y[:],
+                    lhsT=codes[:].bitcast(FP8X4),
+                    lhsT_scale=plane[:],
+                    rhs=words[:].bitcast(FP8X4),
+                    rhs_scale=scales[:],
+                    start=(s == 0),
+                    stop=(s == 1),
+                )
+            return y
+
+        def negated_scores(r, y):
+            neg = tile([P, V], F32, f"neg{r}")
+            nc.vector.scalar_tensor_tensor(
+                out=neg[:], in0=y[:], scalar=-1.0, in1=prior_sb[:], op0=ALU.mult, op1=ALU.subtract
+            )
+            least = tile([P, 1], F32, f"least{r}")
+            nc.vector.tensor_reduce(out=least[:], in_=neg[:], axis=AXIS.X, op=ALU.min)
+            return neg, least
+
+        ys, negs = [], []
+        for r in range(ROWS):
+            ys.append(logs(r))
+            if r >= 1:
+                negs.append(negated_scores(r - 1, ys[r - 1]))
+        negs.append(negated_scores(ROWS - 1, ys[ROWS - 1]))
+
+        for r, (neg, least) in enumerate(negs):
+            ex = tile([P, V], F32, f"ex{r}")
+            total = tile([P, 1], F32, f"total{r}")
+            nc.scalar.activation(out=ex[:], in_=neg[:], func=ACT.Exp, scale=-1.0, bias=least[:], accum_out=total[:])
+            inv = tile([P, 1], F32, f"inv{r}")
+            nc.vector.reciprocal(out=inv[:], in_=total[:])
+            res = tile([P, V], F32, f"res{r}")
+            if r < 2:
+                nc.scalar.activation(out=res[:], in_=ex[:], func=ACT.Copy, scale=inv[:])
+            else:
+                nc.vector.tensor_scalar(out=res[:], in0=ex[:], scalar1=inv[:], scalar2=None, op0=ALU.mult)
+            nc.sync.dma_start(out=out[r * P : (r + 1) * P, :], in_=res[:])

@@ -34,15 +34,12 @@ def tile_picked_ymolrank_post_p_kernel(
         def tile(shape, dtype, name, tag=None):
             return keep.tile(shape, dtype, name=name, tag=tag or name, align_bytes=64)
 
-        offs_sb = tile([P, S // 16], U16, "offs_sb")
-        cand_sb = tile([P, V // 16], U16, "cand_sb")
-
         def words_view(words):
             return words[0].rearrange("p n t -> p (n t)").bitcast(I32)
 
-        def load_scale_rows(queues, table, scales):
-            for quad, queue in enumerate(queues):
-                queue.dma_start(
+        def load_scale_rows(table, scales):
+            for quad in range(4):
+                nc.sync.dma_start(
                     out=table[32 * quad : 32 * quad + 4, :].bitcast(I32),
                     in_=scales[0, 4 * quad : 4 * quad + 4, :].bitcast(I32),
                 )
@@ -52,46 +49,47 @@ def tile_picked_ymolrank_post_p_kernel(
             nc.vector.tensor_copy(out=picked[:], in_=table[:].indirect(offsets))
             return picked
 
+        offs_sb = tile([P, S // 16], U16, "offs_sb")
+        cand_sb = tile([P, V // 16], U16, "cand_sb")
         xs_table = tile([P, T], U8, "xs_table", "scale_rows")
         vs_table = tile([P, G], U8, "vs_table")
-        nc.gpsimd.memset(xs_table[:].bitcast(I32), 0)
-        nc.gpsimd.memset(vs_table[:].bitcast(I32), 0)
+        gs_table = tile([P, G], U8, "gs_table")
+        warm = tile([P, 1], F32, "warm")
+        nc.gpsimd.memset(xs_table[:, : T // 2].bitcast(I32), 0)
+        nc.vector.memset(xs_table[:, T // 2 :].bitcast(I32), 0)
+        nc.vector.memset(warm[:], 0.0)
+        nc.vector.memset(vs_table[:].bitcast(I32), 0)
+        nc.gpsimd.memset(gs_table[:].bitcast(I32), 0)
+        nc.scalar.activation(out=warm[:], in_=warm[:], func=ACT.Tanh)
 
         nc.sync.dma_start(out=offs_sb[:], in_=offs)
         nc.sync.dma_start(out=cand_sb[:], in_=cand)
         w1_rows = w1.rearrange("(p j) c -> p j c", j=PACK)
-        w_raw = [tile([P, PACK, H // 2], F32, f"w_raw{h}", f"stage{h}") for h in range(2)]
-        for h in range(2):
-            nc.scalar.dma_start(out=w_raw[h][:], in_=w1_rows[:, :, h * (H // 2) : (h + 1) * (H // 2)])
-        xw_table = tile([P, T], U32, "xw_table", "wide")
-        nc.scalar.dma_start(out=xw_table[:].bitcast(I32), in_=words_view(x_words))
-        load_scale_rows([nc.sync] * 4, xs_table, x_scales)
-        load_scale_rows([nc.gpsimd, nc.gpsimd, nc.sync, nc.sync], vs_table, v_scales)
-        wpos_sb = tile([P, PACK], F32, "wpos_sb")
-        wneg_sb = tile([P, PACK], F32, "wneg_sb")
-        nc.gpsimd.dma_start(out=wpos_sb[:], in_=wpos.rearrange("(p j) o -> p (j o)", j=PACK))
-        nc.gpsimd.dma_start(out=wneg_sb[:], in_=wneg.rearrange("(p j) o -> p (j o)", j=PACK))
-
-        warm = tile([P, 1], F32, "warm")
-        nc.vector.memset(warm[:], 0.0)
-        nc.scalar.activation(out=warm[:], in_=warm[:], func=ACT.Tanh)
+        w_cuts = (0, H // 4, H)
+        w_raw = [tile([P, PACK, w_cuts[h + 1] - w_cuts[h]], F32, f"w_raw{h}", f"stage{h}") for h in range(2)]
+        nc.sync.dma_start(out=w_raw[0][:], in_=w1_rows[:, :, : w_cuts[1]])
+        load_scale_rows(xs_table, x_scales)
+        nc.sync.dma_start(out=w_raw[1][:], in_=w1_rows[:, :, w_cuts[1] :])
+        load_scale_rows(vs_table, v_scales)
+        xw_table = tile([P, T], U32, "xw_table")
+        nc.sync.dma_start(out=xw_table[:].bitcast(I32), in_=words_view(x_words))
+        load_scale_rows(gs_table, g_scales)
 
         xs = gather("xs", xs_table, offs_sb[:], S, U8)
         vs = gather("vs", vs_table, cand_sb[:], V, U8)
 
-        w_grouped = tile([P, PACK, P, PACK], BF16, "w_grouped")
+        w_grouped = tile([P, PACK, P, PACK], BF16, "w_grouped", "grouped")
         for h in range(2):
             nc.scalar.copy(
-                out=w_grouped[:, :, h * (P // 2) : (h + 1) * (P // 2), :].rearrange("p t m j -> p m t j"),
+                out=w_grouped[:, :, w_cuts[h] // PACK : w_cuts[h + 1] // PACK, :].rearrange("p t m j -> p m t j"),
                 in_=w_raw[h][:].rearrange("p j (m t) -> p m t j", t=PACK),
             )
         vw_table = tile([P, G], U32, "vw_table", "stage0")
         nc.sync.dma_start(out=vw_table[:].bitcast(I32), in_=words_view(v_words))
-        gs_table = tile([P, G], U8, "gs_table", "scale_rows")
-        nc.gpsimd.memset(gs_table[:].bitcast(I32), 0)
-        load_scale_rows([nc.sync] * 4, gs_table, g_scales)
         gw_table = tile([P, G], U32, "gw_table", "stage1")
         nc.sync.dma_start(out=gw_table[:].bitcast(I32), in_=words_view(g_words))
+        prior_table = tile([P, G], F32, "prior_table", "scale_rows")
+        nc.sync.dma_start(out=prior_table[:], in_=prior)
 
         w_codes = tile([P, H], U32, "w_codes")
         w_scales = tile([P, H], U8, "w_scales")
@@ -100,14 +98,14 @@ def tile_picked_ymolrank_post_p_kernel(
             scales=w_scales[:],
             in_=w_grouped[:].rearrange("p t m j -> p (t m j)"),
         )
+        weights = tile([P, 2, 2 * PACK], F32, "weights", "grouped")
+        for s, weight in enumerate((wpos, wneg)):
+            nc.sync.dma_start(out=weights[:, s, :PACK], in_=weight.rearrange("(p j) o -> p (j o)", j=PACK))
 
         xw = [
             gather(f"xw{h}", xw_table, offs_sb[:, h * (HALF // 16) : (h + 1) * (HALF // 16)], HALF, U32)
             for h in range(2)
         ]
-
-        prior_table = tile([P, G], F32, "prior_table", "wide")
-        nc.sync.dma_start(out=prior_table[:], in_=prior)
 
         half_tanh = []
         for r in range(ROWS):
@@ -132,29 +130,37 @@ def tile_picked_ymolrank_post_p_kernel(
         gw = gather("gw", gw_table, cand_sb[:], V, U32)
         prior_sb = gather("prior_sb", prior_table, cand_sb[:], V, F32)
 
-        sides = ((0.5, wpos_sb, vw, vs), (-0.5, wneg_sb, gw, gs))
+        logs = []
+        for r in range(ROWS):
+            lg = tile([P, 2, P, PACK], F32, f"log{r}")
+            for s, slope in enumerate((0.5, -0.5)):
+                nc.scalar.activation(out=lg[:, s], in_=half_tanh[r][:], func=ACT.Ln, scale=slope, bias=0.52)
+            logs.append(lg)
 
-        def logs(r):
-            y = psum.tile([P, V], F32, name=f"y{r}")
-            rounded = []
-            for s, (slope, weight, words, scales) in enumerate(sides):
-                lg = tile([P, P, PACK], F32, f"log{r}_{s}")
-                nc.scalar.activation(out=lg[:], in_=half_tanh[r][:], func=ACT.Ln, scale=slope, bias=0.52)
-                lb = tile([P, P, PACK], BF16, f"lb{r}_{s}")
+        def weighted(r):
+            rounded = tile([P, 2, P, PACK], BF16, f"rounded{r}")
+            for sides in ((slice(0, 1), slice(1, 2)) if r == 0 else (slice(0, 2),)):
+                count = sides.stop - sides.start
                 nc.vector.tensor_tensor(
-                    out=lb[:], in0=lg[:], in1=weight[:].unsqueeze(1).to_broadcast([P, P, PACK]), op=ALU.mult
+                    out=rounded[:, sides],
+                    in0=logs[r][:, sides],
+                    in1=weights[:, sides, :PACK].unsqueeze(2).to_broadcast([P, count, P, PACK]),
+                    op=ALU.mult,
                 )
-                rounded.append(lb)
-            for s, (slope, weight, words, scales) in enumerate(sides):
-                codes = tile([P, P], U32, f"lc{r}_{s}")
-                plane = tile([P, P], U8, f"ls{r}_{s}")
-                nc.vector.quantize_mx(
-                    out=codes[:].bitcast(FP8X4), scales=plane[:], in_=rounded[s][:].rearrange("p n t -> p (n t)")
-                )
+            return rounded
+
+        def scores(r, rounded):
+            codes = tile([P, 2 * P], U32, f"l_codes{r}")
+            plane = tile([P, 2 * P], U8, f"l_scales{r}")
+            nc.vector.quantize_mx(
+                out=codes[:].bitcast(FP8X4), scales=plane[:], in_=rounded[:].rearrange("p s n t -> p (s n t)")
+            )
+            y = psum.tile([P, V], F32, name=f"y{r}")
+            for s, (words, scales) in enumerate(((vw, vs), (gw, gs))):
                 nc.tensor.matmul_mx(
                     out=y[:],
-                    lhsT=codes[:].bitcast(FP8X4),
-                    lhsT_scale=plane[:],
+                    lhsT=codes[:, s * P : (s + 1) * P].bitcast(FP8X4),
+                    lhsT_scale=plane[:, s * P : (s + 1) * P],
                     rhs=words[:].bitcast(FP8X4),
                     rhs_scale=scales[:],
                     start=(s == 0),
@@ -162,31 +168,53 @@ def tile_picked_ymolrank_post_p_kernel(
                 )
             return y
 
-        def negated_scores(r, y):
+        def negated(r, y):
             neg = tile([P, V], F32, f"neg{r}")
             nc.vector.scalar_tensor_tensor(
                 out=neg[:], in0=y[:], scalar=-1.0, in1=prior_sb[:], op0=ALU.mult, op1=ALU.subtract
             )
+            return neg
+
+        def smallest(r, neg):
             least = tile([P, 1], F32, f"least{r}")
             nc.vector.tensor_reduce(out=least[:], in_=neg[:], axis=AXIS.X, op=ALU.min)
-            return neg, least
+            return least
 
-        ys, negs = [], []
-        for r in range(ROWS):
-            ys.append(logs(r))
-            if r >= 1:
-                negs.append(negated_scores(r - 1, ys[r - 1]))
-        negs.append(negated_scores(ROWS - 1, ys[ROWS - 1]))
-
-        for r, (neg, least) in enumerate(negs):
+        def exponentials(r, neg, least):
             ex = tile([P, V], F32, f"ex{r}")
             total = tile([P, 1], F32, f"total{r}")
             nc.scalar.activation(out=ex[:], in_=neg[:], func=ACT.Exp, scale=-1.0, bias=least[:], accum_out=total[:])
+            return ex, total
+
+        def finish(r, ex, total):
             inv = tile([P, 1], F32, f"inv{r}")
             nc.vector.reciprocal(out=inv[:], in_=total[:])
             res = tile([P, V], F32, f"res{r}")
-            if r < 2:
+            if r < ROWS // 2:
                 nc.scalar.activation(out=res[:], in_=ex[:], func=ACT.Copy, scale=inv[:])
             else:
                 nc.vector.tensor_scalar(out=res[:], in0=ex[:], scalar1=inv[:], scalar2=None, op0=ALU.mult)
-            nc.sync.dma_start(out=out[r * P : (r + 1) * P, :], in_=res[:])
+            if r < ROWS - 1:
+                nc.sync.dma_start(out=out[r * P : (r + 1) * P, :], in_=res[:])
+            else:
+                nc.sync.dma_start(out=out[r * P : (r + 1) * P, : V // 2], in_=res[:, : V // 2])
+                nc.scalar.dma_start(out=out[r * P : (r + 1) * P, V // 2 :], in_=res[:, V // 2 :])
+
+        y0 = scores(0, weighted(0))
+        y1 = scores(1, weighted(1))
+        neg0 = negated(0, y0)
+        rounded2 = weighted(2)
+        e0 = exponentials(0, neg0, smallest(0, neg0))
+        y2 = scores(2, rounded2)
+        rounded3 = weighted(3)
+        neg1 = negated(1, y1)
+        y3 = scores(3, rounded3)
+        e1 = exponentials(1, neg1, smallest(1, neg1))
+        finish(0, *e0)
+        neg2 = negated(2, y2)
+        neg3 = negated(3, y3)
+        finish(1, *e1)
+        e2 = exponentials(2, neg2, smallest(2, neg2))
+        e3 = exponentials(3, neg3, smallest(3, neg3))
+        finish(2, *e2)
+        finish(3, *e3)

@@ -1,6 +1,7 @@
 from contextlib import ExitStack
 
 import concourse.mybir as mybir
+from concourse.masks import make_identity
 
 F32 = mybir.dt.float32
 BF16 = mybir.dt.bfloat16
@@ -37,10 +38,10 @@ def tile_picked_ymolrank_post_p_kernel(
         def words_view(words):
             return words[0].rearrange("p n t -> p (n t)").bitcast(I32)
 
-        def load_scale_rows(table, scales):
+        def load_scale_rows(table, scales, first):
             for quad in range(4):
                 nc.sync.dma_start(
-                    out=table[32 * quad : 32 * quad + 4, :].bitcast(I32),
+                    out=table[32 * quad + first : 32 * quad + first + 4, :].bitcast(I32),
                     in_=scales[0, 4 * quad : 4 * quad + 4, :].bitcast(I32),
                 )
 
@@ -54,53 +55,54 @@ def tile_picked_ymolrank_post_p_kernel(
         xs_table = tile([P, T], U8, "xs_table", "scale_rows")
         vs_table = tile([P, G], U8, "vs_table")
         gs_table = tile([P, G], U8, "gs_table")
-        warm = tile([P, 1], F32, "warm")
         nc.gpsimd.memset(xs_table[:, : T // 2].bitcast(I32), 0)
         nc.vector.memset(xs_table[:, T // 2 :].bitcast(I32), 0)
-        nc.vector.memset(warm[:], 0.0)
         nc.vector.memset(vs_table[:].bitcast(I32), 0)
         nc.gpsimd.memset(gs_table[:].bitcast(I32), 0)
-        nc.scalar.activation(out=warm[:], in_=warm[:], func=ACT.Tanh)
+        identity = tile([P, P], F32, "identity")
+        make_identity(nc, identity[:])
 
         nc.sync.dma_start(out=offs_sb[:], in_=offs)
         nc.sync.dma_start(out=cand_sb[:], in_=cand)
         w1_rows = w1.rearrange("(p j) c -> p j c", j=PACK)
         w_cuts = (0, H // 4, H)
-        w_raw = [tile([P, PACK, w_cuts[h + 1] - w_cuts[h]], F32, f"w_raw{h}", f"stage{h}") for h in range(2)]
+        w_raw = [tile([P, PACK, w_cuts[h + 1] - w_cuts[h]], F32, f"w_raw{h}") for h in range(2)]
         nc.sync.dma_start(out=w_raw[0][:], in_=w1_rows[:, :, : w_cuts[1]])
-        load_scale_rows(xs_table, x_scales)
+        load_scale_rows(xs_table, x_scales, 0)
         nc.sync.dma_start(out=w_raw[1][:], in_=w1_rows[:, :, w_cuts[1] :])
-        load_scale_rows(vs_table, v_scales)
+        load_scale_rows(vs_table, v_scales, 4)
         xw_table = tile([P, T], U32, "xw_table")
         nc.sync.dma_start(out=xw_table[:].bitcast(I32), in_=words_view(x_words))
-        load_scale_rows(gs_table, g_scales)
+        load_scale_rows(gs_table, g_scales, 8)
+        vw_table = tile([P, G], U32, "vw_table")
+        nc.sync.dma_start(out=vw_table[:].bitcast(I32), in_=words_view(v_words))
+        gw_table = tile([P, G], U32, "gw_table")
+        nc.sync.dma_start(out=gw_table[:].bitcast(I32), in_=words_view(g_words))
+        prior_table = tile([P, G], F32, "prior_table")
+        nc.sync.dma_start(out=prior_table[:], in_=prior)
+        weights = tile([P, 2, 2 * PACK], F32, "weights")
+        for s, weight in enumerate((wpos, wneg)):
+            nc.gpsimd.dma_start(out=weights[:, s, :PACK], in_=weight.rearrange("(p j) o -> p (j o)", j=PACK))
 
         xs = gather("xs", xs_table, offs_sb[:], S, U8)
         vs = gather("vs", vs_table, cand_sb[:], V, U8)
 
         w_grouped = tile([P, PACK, P, PACK], BF16, "w_grouped", "grouped")
-        for h in range(2):
-            nc.scalar.copy(
-                out=w_grouped[:, :, w_cuts[h] // PACK : w_cuts[h + 1] // PACK, :].rearrange("p t m j -> p m t j"),
-                in_=w_raw[h][:].rearrange("p j (m t) -> p m t j", t=PACK),
-            )
-        vw_table = tile([P, G], U32, "vw_table", "stage0")
-        nc.sync.dma_start(out=vw_table[:].bitcast(I32), in_=words_view(v_words))
-        gw_table = tile([P, G], U32, "gw_table", "stage1")
-        nc.sync.dma_start(out=gw_table[:].bitcast(I32), in_=words_view(g_words))
-        prior_table = tile([P, G], F32, "prior_table", "scale_rows")
-        nc.sync.dma_start(out=prior_table[:], in_=prior)
+        for h, lo, hi in ((0, 0, 128), (1, 128, 384), (1, 384, 512)):
+            src = w_raw[h][:, :, lo - w_cuts[h] : hi - w_cuts[h]].rearrange("p j (m t) -> p m t j", t=PACK)
+            dst = w_grouped[:, :, lo // PACK : hi // PACK, :].rearrange("p t m j -> p m t j")
+            if hi < H:
+                nc.scalar.activation(out=dst, in_=src, func=ACT.Copy)
+            else:
+                nc.vector.tensor_copy(out=dst, in_=src)
 
         w_codes = tile([P, H], U32, "w_codes")
-        w_scales = tile([P, H], U8, "w_scales")
+        w_scales = tile([P, H], U8, "w_scales", "vs_table")
         nc.vector.quantize_mx(
             out=w_codes[:].bitcast(FP8X4),
             scales=w_scales[:],
             in_=w_grouped[:].rearrange("p t m j -> p (t m j)"),
         )
-        weights = tile([P, 2, 2 * PACK], F32, "weights", "grouped")
-        for s, weight in enumerate((wpos, wneg)):
-            nc.sync.dma_start(out=weights[:, s, :PACK], in_=weight.rearrange("(p j) o -> p (j o)", j=PACK))
 
         xw = [
             gather(f"xw{h}", xw_table, offs_sb[:, h * (HALF // 16) : (h + 1) * (HALF // 16)], HALF, U32)
@@ -137,8 +139,7 @@ def tile_picked_ymolrank_post_p_kernel(
                 nc.scalar.activation(out=lg[:, s], in_=half_tanh[r][:], func=ACT.Ln, scale=slope, bias=0.52)
             logs.append(lg)
 
-        def weighted(r):
-            rounded = tile([P, 2, P, PACK], BF16, f"rounded{r}")
+        def weigh(r, rounded):
             for sides in ((slice(0, 1), slice(1, 2)) if r == 0 else (slice(0, 2),)):
                 count = sides.stop - sides.start
                 nc.vector.tensor_tensor(
@@ -147,26 +148,68 @@ def tile_picked_ymolrank_post_p_kernel(
                     in1=weights[:, sides, :PACK].unsqueeze(2).to_broadcast([P, count, P, PACK]),
                     op=ALU.mult,
                 )
-            return rounded
 
-        def scores(r, rounded):
-            codes = tile([P, 2 * P], U32, f"l_codes{r}")
-            plane = tile([P, 2 * P], U8, f"l_scales{r}")
+        def quantised(name, rounded, width):
+            codes = tile([P, 2, width], U32, f"l_codes{name}")
+            plane = tile([P, 2, width], U8, f"l_scales{name}")
             nc.vector.quantize_mx(
-                out=codes[:].bitcast(FP8X4), scales=plane[:], in_=rounded[:].rearrange("p s n t -> p (s n t)")
+                out=codes[:].rearrange("p s n -> p (s n)").bitcast(FP8X4),
+                scales=plane[:].rearrange("p s n -> p (s n)"),
+                in_=rounded[:].rearrange("p s n t -> p (s n t)"),
             )
+            return codes, plane
+
+        stores = ((vw, vs, 4), (gw, gs, 8))
+
+        prior_turned = psum.tile([P, V // P, P], F32, name="prior_turned", tag="z0")
+        for b in range(V // P):
+            nc.tensor.transpose(prior_turned[:, b, :], prior_sb[:, b * P : (b + 1) * P], identity[:])
+        neg_prior = tile([P, V // P], F32, "neg_prior")
+        nc.vector.tensor_scalar(out=neg_prior[:], in0=prior_turned[:, :, 0], scalar1=-1.0, scalar2=None, op0=ALU.mult)
+
+        negs = []
+        for r in range(2):
+            rounded = tile([P, 2, P, PACK], BF16, f"rounded{r}", "prior_table" if r == 0 else None)
+            weigh(r, rounded[:])
+            codes, plane = quantised(r, rounded, P)
+            turned = psum.tile([P, V // P, P], F32, name=f"turned{r}", tag=f"z{r + 1}")
+            for b in range(V // P):
+                for s, (words, scales, first) in enumerate(stores):
+                    nc.tensor.matmul_mx(
+                        out=turned[:, b, :],
+                        lhsT=words[:, b * P : (b + 1) * P].bitcast(FP8X4),
+                        lhsT_scale=scales[first:, b * P : (b + 1) * P],
+                        rhs=codes[:, s, :].bitcast(FP8X4),
+                        rhs_scale=plane[:, s, :],
+                        start=(s == 0),
+                        stop=(s == 1),
+                    )
+            held = tile([P, V // P, P], F32, f"held{r}")
+            neg = psum.tile([P, V], F32, name=f"y{r}")
+            for b in range(V // P):
+                nc.scalar.activation(
+                    out=held[:, b, :], in_=turned[:, b, :], func=ACT.Identity, scale=-1.0, bias=neg_prior[:, b : b + 1]
+                )
+                nc.tensor.transpose(neg[:, b * P : (b + 1) * P], held[:, b, :], identity[:])
+            negs.append(neg)
+
+        ys = []
+        for r in (2, 3):
+            rounded = tile([P, 2, P, PACK], BF16, f"rounded{r}")
+            weigh(r, rounded[:])
+            codes, plane = quantised(r, rounded, P)
             y = psum.tile([P, V], F32, name=f"y{r}")
-            for s, (words, scales) in enumerate(((vw, vs), (gw, gs))):
+            for s, (words, scales, first) in enumerate(stores):
                 nc.tensor.matmul_mx(
                     out=y[:],
-                    lhsT=codes[:, s * P : (s + 1) * P].bitcast(FP8X4),
-                    lhsT_scale=plane[:, s * P : (s + 1) * P],
+                    lhsT=codes[:, s, :].bitcast(FP8X4),
+                    lhsT_scale=plane[:, s, :],
                     rhs=words[:].bitcast(FP8X4),
-                    rhs_scale=scales[:],
+                    rhs_scale=scales[first:, :],
                     start=(s == 0),
                     stop=(s == 1),
                 )
-            return y
+            ys.append(y)
 
         def negated(r, y):
             neg = tile([P, V], F32, f"neg{r}")
@@ -175,12 +218,9 @@ def tile_picked_ymolrank_post_p_kernel(
             )
             return neg
 
-        def smallest(r, neg):
-            least = tile([P, 1], F32, f"least{r}")
+        def exponentials(r, neg):
+            least = tile([P, 1], F32, f"least{r}", "rounded3" if r == 0 else None)
             nc.vector.tensor_reduce(out=least[:], in_=neg[:], axis=AXIS.X, op=ALU.min)
-            return least
-
-        def exponentials(r, neg, least):
             ex = tile([P, V], F32, f"ex{r}")
             total = tile([P, 1], F32, f"total{r}")
             nc.scalar.activation(out=ex[:], in_=neg[:], func=ACT.Exp, scale=-1.0, bias=least[:], accum_out=total[:])
@@ -190,8 +230,8 @@ def tile_picked_ymolrank_post_p_kernel(
             inv = tile([P, 1], F32, f"inv{r}")
             nc.vector.reciprocal(out=inv[:], in_=total[:])
             res = tile([P, V], F32, f"res{r}")
-            if r < ROWS // 2:
-                nc.scalar.activation(out=res[:], in_=ex[:], func=ACT.Copy, scale=inv[:])
+            if r < 2:
+                nc.gpsimd.tensor_scalar(out=res[:], in0=ex[:], scalar1=inv[:], scalar2=0.0, op0=ALU.mult, op1=ALU.add)
             else:
                 nc.vector.tensor_scalar(out=res[:], in0=ex[:], scalar1=inv[:], scalar2=None, op0=ALU.mult)
             if r < ROWS - 1:
@@ -200,21 +240,13 @@ def tile_picked_ymolrank_post_p_kernel(
                 nc.sync.dma_start(out=out[r * P : (r + 1) * P, : V // 2], in_=res[:, : V // 2])
                 nc.scalar.dma_start(out=out[r * P : (r + 1) * P, V // 2 :], in_=res[:, V // 2 :])
 
-        y0 = scores(0, weighted(0))
-        y1 = scores(1, weighted(1))
-        neg0 = negated(0, y0)
-        rounded2 = weighted(2)
-        e0 = exponentials(0, neg0, smallest(0, neg0))
-        y2 = scores(2, rounded2)
-        rounded3 = weighted(3)
-        neg1 = negated(1, y1)
-        y3 = scores(3, rounded3)
-        e1 = exponentials(1, neg1, smallest(1, neg1))
+        e0 = exponentials(0, negs[0])
+        neg2 = negated(2, ys[0])
+        e1 = exponentials(1, negs[1])
         finish(0, *e0)
-        neg2 = negated(2, y2)
-        neg3 = negated(3, y3)
+        neg3 = negated(3, ys[1])
         finish(1, *e1)
-        e2 = exponentials(2, neg2, smallest(2, neg2))
-        e3 = exponentials(3, neg3, smallest(3, neg3))
+        e2 = exponentials(2, neg2)
+        e3 = exponentials(3, neg3)
         finish(2, *e2)
         finish(3, *e3)

from contextlib import ExitStack

import concourse.mybir as mybir
from concourse.masks import make_identity

F32 = mybir.dt.float32
BF16 = mybir.dt.bfloat16
I32 = mybir.dt.int32
U32 = mybir.dt.uint32
U16 = mybir.dt.uint16
U8 = mybir.dt.uint8
FP8X4 = mybir.dt.float8_e4m3fn_x4
ACT = mybir.ActivationFunctionType
ALU = mybir.AluOpType
AXIS = mybir.AxisListType

P = 128
PACK = 4
K, T, S, H, G, V = 512, 2048, 512, 512, 1024, 512
ROWS = S // P
HALF = S // 2

FLOPS = 2 * K * H * S + 2 * 2 * H * S * V
BYTES = 4 * (K * H + 2 * H + G + S * V) + (K + K // 32) * S + 2 * (H + H // 32) * V + 2 * (S + V)


def tile_picked_ymolrank_post_p_kernel(
    tc, x_words, x_scales, w1, wpos, wneg, v_words, v_scales, g_words, g_scales, prior, offs, cand, out
):
    nc = tc.nc
    with ExitStack() as ctx:
        keep = ctx.enter_context(tc.tile_pool(name="keep", bufs=1))
        psum = ctx.enter_context(tc.psum_pool(name="psum", bufs=1))

        def tile(shape, dtype, name, tag=None):
            return keep.tile(shape, dtype, name=name, tag=tag or name, align_bytes=64)

        def words_view(words):
            return words[0].rearrange("p n t -> p (n t)").bitcast(I32)

        def load_scale_rows(table, scales, first):
            for quad in range(4):
                nc.sync.dma_start(
                    out=table[32 * quad + first : 32 * quad + first + 4, :].bitcast(I32),
                    in_=scales[0, 4 * quad : 4 * quad + 4, :].bitcast(I32),
                )

        def gather(name, table, offsets, count, dtype):
            picked = tile([P, count], dtype, name)
            nc.vector.tensor_copy(out=picked[:], in_=table[:].indirect(offsets))
            return picked

        offs_sb = tile([P, S // 16], U16, "offs_sb")
        cand_sb = tile([P, V // 16], U16, "cand_sb")
        xs_table = tile([P, T], U8, "xs_table", "scale_rows")
        vs_table = tile([P, G], U8, "vs_table")
        gs_table = tile([P, G], U8, "gs_table")
        nc.gpsimd.memset(xs_table[:, : T // 2].bitcast(I32), 0)
        nc.vector.memset(xs_table[:, T // 2 :].bitcast(I32), 0)
        nc.vector.memset(vs_table[:].bitcast(I32), 0)
        nc.gpsimd.memset(gs_table[:].bitcast(I32), 0)
        identity = tile([P, P], F32, "identity")
        make_identity(nc, identity[:])

        nc.sync.dma_start(out=offs_sb[:], in_=offs)
        nc.sync.dma_start(out=cand_sb[:], in_=cand)
        w1_rows = w1.rearrange("(p j) c -> p j c", j=PACK)
        w_cuts = (0, H // 4, H)
        w_raw = [tile([P, PACK, w_cuts[h + 1] - w_cuts[h]], F32, f"w_raw{h}") for h in range(2)]
        nc.sync.dma_start(out=w_raw[0][:], in_=w1_rows[:, :, : w_cuts[1]])
        load_scale_rows(xs_table, x_scales, 0)
        nc.sync.dma_start(out=w_raw[1][:], in_=w1_rows[:, :, w_cuts[1] :])
        load_scale_rows(vs_table, v_scales, 4)
        xw_table = tile([P, T], U32, "xw_table")
        nc.sync.dma_start(out=xw_table[:].bitcast(I32), in_=words_view(x_words))
        load_scale_rows(gs_table, g_scales, 8)
        vw_table = tile([P, G], U32, "vw_table")
        nc.sync.dma_start(out=vw_table[:].bitcast(I32), in_=words_view(v_words))
        gw_table = tile([P, G], U32, "gw_table")
        nc.sync.dma_start(out=gw_table[:].bitcast(I32), in_=words_view(g_words))
        prior_table = tile([P, G], F32, "prior_table")
        nc.sync.dma_start(out=prior_table[:], in_=prior)
        weights = tile([P, 2, 2 * PACK], F32, "weights")
        for s, weight in enumerate((wpos, wneg)):
            nc.gpsimd.dma_start(out=weights[:, s, :PACK], in_=weight.rearrange("(p j) o -> p (j o)", j=PACK))

        xs = gather("xs", xs_table, offs_sb[:], S, U8)
        vs = gather("vs", vs_table, cand_sb[:], V, U8)

        w_grouped = tile([P, PACK, P, PACK], BF16, "w_grouped", "grouped")
        for h, lo, hi in ((0, 0, 128), (1, 128, 384), (1, 384, 512)):
            src = w_raw[h][:, :, lo - w_cuts[h] : hi - w_cuts[h]].rearrange("p j (m t) -> p m t j", t=PACK)
            dst = w_grouped[:, :, lo // PACK : hi // PACK, :].rearrange("p t m j -> p m t j")
            if hi < H:
                nc.scalar.activation(out=dst, in_=src, func=ACT.Copy)
            else:
                nc.vector.tensor_copy(out=dst, in_=src)

        w_codes = tile([P, H], U32, "w_codes")
        w_scales = tile([P, H], U8, "w_scales", "vs_table")
        nc.vector.quantize_mx(
            out=w_codes[:].bitcast(FP8X4),
            scales=w_scales[:],
            in_=w_grouped[:].rearrange("p t m j -> p (t m j)"),
        )

        xw = [
            gather(f"xw{h}", xw_table, offs_sb[:, h * (HALF // 16) : (h + 1) * (HALF // 16)], HALF, U32)
            for h in range(2)
        ]

        half_tanh = []
        for r in range(ROWS):
            z = psum.tile([P, PACK, P], F32, name=f"z{r}")
            h, lo = divmod(r * P, HALF)
            for t in range(PACK):
                nc.tensor.matmul_mx(
                    out=z[:, t, :],
                    lhsT=w_codes[:, t * P : (t + 1) * P].bitcast(FP8X4),
                    lhsT_scale=w_scales[:, t * P : (t + 1) * P],
                    rhs=xw[h][:, lo : lo + P].bitcast(FP8X4),
                    rhs_scale=xs[:, r * P : (r + 1) * P],
                    start=True,
                    stop=True,
                )
            th = tile([P, P, PACK], F32, f"th{r}")
            nc.scalar.activation(out=th[:], in_=z[:].rearrange("p t n -> p n t"), func=ACT.Tanh, scale=0.5)
            half_tanh.append(th)

        gs = gather("gs", gs_table, cand_sb[:], V, U8)
        vw = gather("vw", vw_table, cand_sb[:], V, U32)
        gw = gather("gw", gw_table, cand_sb[:], V, U32)
        prior_sb = gather("prior_sb", prior_table, cand_sb[:], V, F32)

        logs = []
        for r in range(ROWS):
            lg = tile([P, 2, P, PACK], F32, f"log{r}")
            for s, slope in enumerate((0.5, -0.5)):
                nc.scalar.activation(out=lg[:, s], in_=half_tanh[r][:], func=ACT.Ln, scale=slope, bias=0.52)
            logs.append(lg)

        def weigh(r, rounded):
            for sides in ((slice(0, 1), slice(1, 2)) if r == 0 else (slice(0, 2),)):
                count = sides.stop - sides.start
                nc.vector.tensor_tensor(
                    out=rounded[:, sides],
                    in0=logs[r][:, sides],
                    in1=weights[:, sides, :PACK].unsqueeze(2).to_broadcast([P, count, P, PACK]),
                    op=ALU.mult,
                )

        def quantised(name, rounded, width):
            codes = tile([P, 2, width], U32, f"l_codes{name}")
            plane = tile([P, 2, width], U8, f"l_scales{name}")
            nc.vector.quantize_mx(
                out=codes[:].rearrange("p s n -> p (s n)").bitcast(FP8X4),
                scales=plane[:].rearrange("p s n -> p (s n)"),
                in_=rounded[:].rearrange("p s n t -> p (s n t)"),
            )
            return codes, plane

        stores = ((vw, vs, 4), (gw, gs, 8))

        prior_turned = psum.tile([P, V // P, P], F32, name="prior_turned", tag="z0")
        for b in range(V // P):
            nc.tensor.transpose(prior_turned[:, b, :], prior_sb[:, b * P : (b + 1) * P], identity[:])
        neg_prior = tile([P, V // P], F32, "neg_prior")
        nc.vector.tensor_scalar(out=neg_prior[:], in0=prior_turned[:, :, 0], scalar1=-1.0, scalar2=None, op0=ALU.mult)

        negs = []
        for r in range(2):
            rounded = tile([P, 2, P, PACK], BF16, f"rounded{r}", "prior_table" if r == 0 else None)
            weigh(r, rounded[:])
            codes, plane = quantised(r, rounded, P)
            turned = psum.tile([P, V // P, P], F32, name=f"turned{r}", tag=f"z{r + 1}")
            for b in range(V // P):
                for s, (words, scales, first) in enumerate(stores):
                    nc.tensor.matmul_mx(
                        out=turned[:, b, :],
                        lhsT=words[:, b * P : (b + 1) * P].bitcast(FP8X4),
                        lhsT_scale=scales[first:, b * P : (b + 1) * P],
                        rhs=codes[:, s, :].bitcast(FP8X4),
                        rhs_scale=plane[:, s, :],
                        start=(s == 0),
                        stop=(s == 1),
                    )
            held = tile([P, V // P, P], F32, f"held{r}")
            neg = psum.tile([P, V], F32, name=f"y{r}")
            for b in range(V // P):
                nc.scalar.activation(
                    out=held[:, b, :], in_=turned[:, b, :], func=ACT.Identity, scale=-1.0, bias=neg_prior[:, b : b + 1]
                )
                nc.tensor.transpose(neg[:, b * P : (b + 1) * P], held[:, b, :], identity[:])
            negs.append(neg)

        ys = []
        for r in (2, 3):
            rounded = tile([P, 2, P, PACK], BF16, f"rounded{r}")
            weigh(r, rounded[:])
            codes, plane = quantised(r, rounded, P)
            y = psum.tile([P, V], F32, name=f"y{r}")
            for s, (words, scales, first) in enumerate(stores):
                nc.tensor.matmul_mx(
                    out=y[:],
                    lhsT=codes[:, s, :].bitcast(FP8X4),
                    lhsT_scale=plane[:, s, :],
                    rhs=words[:].bitcast(FP8X4),
                    rhs_scale=scales[first:, :],
                    start=(s == 0),
                    stop=(s == 1),
                )
            ys.append(y)

        def negated(r, y):
            neg = tile([P, V], F32, f"neg{r}")
            nc.vector.scalar_tensor_tensor(
                out=neg[:], in0=y[:], scalar=-1.0, in1=prior_sb[:], op0=ALU.mult, op1=ALU.subtract
            )
            return neg

        def exponentials(r, neg):
            least = tile([P, 1], F32, f"least{r}", "rounded3" if r == 0 else None)
            nc.vector.tensor_reduce(out=least[:], in_=neg[:], axis=AXIS.X, op=ALU.min)
            ex = tile([P, V], F32, f"ex{r}")
            total = tile([P, 1], F32, f"total{r}")
            nc.scalar.activation(out=ex[:], in_=neg[:], func=ACT.Exp, scale=-1.0, bias=least[:], accum_out=total[:])
            return ex, total

        def finish(r, ex, total):
            inv = tile([P, 1], F32, f"inv{r}")
            nc.vector.reciprocal(out=inv[:], in_=total[:])
            res = tile([P, V], F32, f"res{r}")
            if r < 2:
                nc.gpsimd.tensor_scalar(out=res[:], in0=ex[:], scalar1=inv[:], scalar2=0.0, op0=ALU.mult, op1=ALU.add)
            else:
                nc.vector.tensor_scalar(out=res[:], in0=ex[:], scalar1=inv[:], scalar2=None, op0=ALU.mult)
            if r < ROWS - 1:
                nc.sync.dma_start(out=out[r * P : (r + 1) * P, :], in_=res[:])
            else:
                nc.sync.dma_start(out=out[r * P : (r + 1) * P, : V // 2], in_=res[:, : V // 2])
                nc.scalar.dma_start(out=out[r * P : (r + 1) * P, V // 2 :], in_=res[:, V // 2 :])

        e0 = exponentials(0, negs[0])
        neg2 = negated(2, ys[0])
        e1 = exponentials(1, negs[1])
        finish(0, *e0)
        neg3 = negated(3, ys[1])
        finish(1, *e1)
        e2 = exponentials(2, neg2)
        e3 = exponentials(3, neg3)
        finish(2, *e2)
        finish(3, *e3)
